import numpy as np, ml_dtypes
CORES = [2,6,10,14,18,22,26,30]
N = 8
BF = ml_dtypes.bfloat16
W, P, Q, C, R, EV = 4096, 11, 192, 48, 2, 1024
def spots(e, w):
    a = np.sum(w[..., 0:1] * e, axis=-2) & 4095; b = np.sum(w[..., 1:2] * e, axis=-2) & 4095; m = a * b
    return ((m >> 5) + b) & (W - 1), ((m >> 9) + a) & (W - 1), (m >> 7) & (EV - 1)
def lattice():
    i = np.stack(np.meshgrid(*[np.arange(17)] * 4, indexing="ij"), -1).reshape(-1, 4)
    i = i[np.all(i[:, 1:] >= i[:, :-1], axis=1)]; v = np.zeros((len(i), 17), np.int64)
    np.add.at(v, (np.arange(len(i))[:, None], i), 1)
    return np.concatenate([v[:, :16], (np.arange(5, 201)[:, None, None] * np.eye(16, dtype=np.int64)).reshape(-1, 16)])
LST = lattice()
def place(e, w):
    h1, h2, z = spots(e.T, w); odd = (z & 1) == 1; at = np.full(len(e), -1, np.int64); used = np.zeros(W, bool)
    for h in (np.where(odd, h2, h1), np.where(odd, h1, h2)):
        o = np.flatnonzero((at < 0) & ~used[h]); i = o[np.unique(h[o], return_index=True)[1]]
        at[i] = h[i]; used[h[i]] = True
    return at
def seat(rng, e):
    for i in range(50):
        w = rng.integers(1, 4096, (16, 2))
        if np.min(place(e, w)) >= 0: break
    return w
def tab(rng, a, n, act, far):
    e = LST[np.argsort(np.dot(LST, a))[:n]]; x = rng.integers(0, 201, (far, 16)); t = rng.permutation(far)
    x[:, 0] = rng.integers(100, 201, far); x[:, 1] = t % 200; x[:, 2] = t // 200; x[:, 3] = np.maximum(x[:, 3], 1)
    k = np.full(n + far, 2, np.int64); lo = n - max(act, n // 3); k[lo + rng.permutation(n - lo)[:act]] = 1
    k[n:] = 1 + (rng.random(far) < 0.5)
    sz = np.concatenate([rng.integers(64, 257, n), rng.integers(8, 33, far)])
    return np.concatenate([e, x]), k, (sz[:, None] * rng.random((n + far, 16))).astype(np.int64)
def plain(rng, r, a, young):
    a = a * (1 + 0.02 * rng.random(16))
    if young: return tab(rng, a, 17, 16, 2 * Q)
    return tab(rng, a, W // 3 - r * (W // 64) + int(rng.integers(0, W // 128)), W // 34, W // 10)
def pack(rng, w, items, nq, th, env=None, stray=0.0):
    ex = np.full((N, 8, 16, W), -1, np.int32); su = np.zeros((N, 8, 16, W), np.int32); st = np.zeros((N, 8, W), np.int32); qu = np.full((N, 8, Q), -1, np.int32)
    for r in range(N):
        for g in range(8):
            e, k, s, *out = items[r][g]; out = out[0] if out else rng.random(len(e)) < stray
            at = place(e, w[r, g]); i = np.flatnonzero(at >= 0); p = at[i]
            if np.any(out):
                h1, h2, z = spots(e.T, w[r, g]); free = rng.permutation(np.setdiff1d(np.arange(W), p))
                j = np.flatnonzero(out[i])[:len(free)]; to = free[:len(j)]
                away = (to != h1[i[j]]) & (to != h2[i[j]]); p[j[away]] = to[away]
            ex[r, g][:, p] = e[i].T; su[r, g][:, p] = s[i].T; st[r, g, p] = k[i]
            o = rng.permutation(p[k[i] == 1][:int(nq[r, g])]); qu[r, g, :len(o)] = o
    if env is None: env = rng.integers(0, 256, (N, 128, EV))
    return {"ex": ex.reshape(N, 128, W).astype(np.float32).astype(BF), "su": su.reshape(N, 128, W).astype(np.float32).astype(BF), "st": st, "qu": qu,
            "wt": np.ascontiguousarray(w.reshape(N, 128, 2)).astype(np.int32), "env": env.astype(np.float32).astype(BF), "th": np.ascontiguousarray(th.reshape(N, 8, 1)).astype(np.int32)}
def parts(rng):
    w = rng.integers(1, 4096, (N, 8, 16, 2)); a = 1 + 0.9 * rng.random((8, 16)); th = rng.integers(150, 700, (N, 8))
    y = (int(rng.integers(0, 8)) + 3 * np.arange(N)) % 8
    items = [[plain(rng, r, a[g], g == y[r]) for g in range(8)] for r in range(N)]
    nq = rng.integers(Q // 2, Q + 1, (N, 8))
    for r in range(N): nq[r, y[r]] = Q; nq[r, (y[r] + 4) % 8] = rng.integers(0, P)
    return w, a, th, items, nq
def setup_inputs(rng):
    w, a, th, items, nq = parts(rng)
    return pack(rng, w, items, nq, th)
def exact(rng, want):
    m = 1
    while m * m < want: m += 1
    x = m * m - want; o = rng.permutation(16); o[:m] = np.sort(o[:m]); one = np.eye(16, dtype=np.int64)[o]
    pairs = np.array([(i, j) for i in range(m) for j in range(i)], np.int64).reshape(-1, 2); pairs = pairs[rng.permutation(len(pairs))[:x // 2]]
    e = np.concatenate([np.zeros((1, 16), np.int64), one, one[pairs[:, 0]] + one[pairs[:, 1]], 2 * one[:x % 2]])
    k = np.full(len(e), 2, np.int64); k[1:17] = 1; s = np.zeros((len(e), 16), np.int64)
    s[0] = rng.integers(0, 256, 16); s[1:m] = rng.integers(129, 256, (m - 1, 16)); s[m] = 128
    return (e, k, s), seat(rng, e)
def setup_inputs_room(rng):
    w, a, th, items, nq = parts(rng); a = 1 + 0.01 * rng.random((8, 16))
    for r in range(N):
        for g in range(8):
            items[r][g] = plain(rng, r, a[g], r % 2 == 1 and g in (3, 6)); nq[r, g] = Q
            if r % 2 == 1 and g in (0, 1, 2, 4):
                items[r][g], w[r, g] = exact(rng, {0: C, 1: C + 1, 2: C - 1, 4: 1}[g]); th[r, g] = 1000
            if r % 2 == 1 and g in (3, 6): th[r, g] = 200
            if r % 2 == 0 and g == 6:
                e, k, s = items[r][g]; two = rng.permutation(np.flatnonzero(np.sum(e, axis=1) == 2))[:P + 4]
                k[two] = 1; s[two] = 255
    return pack(rng, w, items, nq, th)
def setup_inputs_ties(rng):
    w, a, th, items, nq = parts(rng); th = rng.choice(np.array([512, 512, 513, 1024]), (N, 8))
    for r in range(N):
        for g in range(8):
            e, k, s = items[r][g]; v = rng.choice(np.array([32, 64, 64]), (len(e), 1))
            items[r][g] = e, k, np.tile(v, (1, 16))
    e = np.concatenate([np.zeros((1, 16), np.int64), np.eye(16, dtype=np.int64)]); k = np.full(17, 1, np.int64); k[0] = 2
    items[0][0] = e, k, np.full((17, 16), 64, np.int64); w[0, 0] = seat(rng, e); nq[0, 0] = Q; th[0, 0] = 1024
    return pack(rng, w, items, nq, th, 128 * rng.integers(0, 2, (N, 128, EV)))
def forge(rng):
    b = np.concatenate([np.array([5, 5]), rng.integers(2, 121, 2), np.array([5]), rng.integers(2, 121, 3)])
    n = np.arange(8); u = 2 * n + (n > 3); v = 4 * n + 1 - u; one = np.eye(16, dtype=np.int64); es = []; ks = []
    for j in range(11):
        p = j if j < 8 else (0, 1, int(rng.integers(2, 8)))[j - 8]
        x = (2 * p + 2 + int(rng.integers(0, 14))) % 16; y = np.zeros(16, np.int64)
        y[u[p]] = rng.integers(2, 61); y[v[p]] = rng.integers(4, 61); y[x] = 10 * j + 5 + rng.integers(0, 4)
        near = y - one[np.array([u[p], v[p], x])]; more = b[p] * one[u[p]] - one[v[p]]
        if j < 8: near[2] = near[2] + more
        else: near = np.concatenate([near, (y + more)[None]])
        k = np.full(len(near), 2, np.int64); k[0] = 1; es.append(near); ks.append(k)
    return np.concatenate(es), np.concatenate(ks), b, u, v
def setup_inputs_clash(rng):
    w, a, th, items, nq = parts(rng); th = rng.integers(100, 300, (N, 8))
    for r in range(N):
        for g in range(8): items[r][g] = plain(rng, r, a[g], r % 2 == 1 and 1 <= g <= 4); nq[r, g] = Q
        if r % 2 == 1:
            w[r, 1, :, 0] = 0; w[r, 2, :, 1] = w[r, 2, :, 0]; w[r, 3, :, 1] = 0; w[r, 4, 1::2] = w[r, 4, ::2]
            few = rng.choice(np.array([0, 1, 2, 64, 2048, 4095]), (3, 16, 2)); w[r, 5:] = np.where(rng.random((3, 16, 2)) < 0.5, few, w[r, 5:])
    e, k, b, u, v = forge(rng)
    for r in range(N):
        w[r, 0, v] = (b[:, None] * w[r, 0, u]) & 4095; items[r][0] = e, k, rng.integers(100, 256, (len(e), 16))
    return pack(rng, w, items, nq, th)
def dense(rng, n):
    y = rng.integers(100, 201, (n, 16)); y[1::2] = rng.integers(1, 4, y[1::2].shape); y[:, 0] = 100 + 3 * rng.permutation(33)[:n]
    return y
def kin(rng, y, j):
    s = 80 + 8 * np.arange(16)[:, None] + rng.integers(0, 56, (16, 16))
    return y - np.eye(16, dtype=np.int64), np.full(16, 2, np.int64), s[::-1] if j % 2 == 0 else s, np.zeros(16, bool)
def nest(l, w):
    e, k, s, out = [np.concatenate(v) for v in zip(*l)]
    if np.any(e[0] != 0):
        h1, h2, z = spots(e.T, w); i = (h1 > 0) & (h2 > 0); e, k, s, out = e[i], k[i], s[i], out[i]
    return e, k, s, out
def setup_inputs_short(rng):
    w, a, th, items, nq = parts(rng); nq = rng.choice(np.array([0, 1, P - 1, P, P + 1, Q]), (N, 8))
    nq[0] = np.array([0, 1, P - 1, P, P + 1, 1, Q, Q]); nq[1, 0] = Q; nq[N - 1] = 0; nq[::2, 5] = 1; nq[:N - 1, 6] = Q; nq[:, 7] = Q
    th[:, 5] = 100; th[:, 6:] = rng.integers(50, 300, (N, 2))
    y = dense(rng, 6); b = dense(rng, 4 * N).reshape(N, 4, 16)
    for r in range(N):
        if r % 2 == 1: items[r][5] = tab(rng, a[5], 0, 0, 0)
        else: items[r][5] = np.zeros((1, 16), np.int64), np.ones(1, np.int64), rng.integers(64, 256, (1, 16))
        z = [(np.zeros((1, 16), np.int64), np.full(1, 2, np.int64), rng.integers(200, 256, (1, 16)), np.zeros(1, bool))] if r % 2 == 0 else []
        l = []
        for j in range(6):
            e, k, s, out = kin(rng, y[j], j); k[int(rng.integers(0, 16 if j < 4 else 7))] = 1
            i = np.flatnonzero(np.arange(16) != {4: 15, 5: 7}.get(j, 16)); l.append((e[i], k[i], s[i], out[i]))
        items[r][6] = nest(z + l, w[r, 6])
        l = [(b[r], np.ones(4, np.int64), rng.integers(150, 256, (4, 16)), np.arange(4) == 1)] + [kin(rng, b[r - 1, j], j) for j in range(4)]
        l.append((b[r - 1, 2:3], np.full(1, 2, np.int64), rng.integers(64, 256, (1, 16)), np.zeros(1, bool)))
        items[r][7] = nest(z + l, w[r, 7])
    return pack(rng, w, items, nq, th)
def setup_inputs_spread(rng):
    w, a, th, items, nq = parts(rng); w = rng.integers(0, 4096, (N, 8, 16, 2)); w[:, :, 3] = 4095
    a = np.exp2(-2 + 3 * rng.random((8, 16))); a[0, 0] = 0.001
    th = np.minimum(np.exp2(12 * rng.random((N, 8))).astype(np.int64), 4080)
    for r in range(N):
        for g in range(8):
            if r % 2 == 1 and g == 6: continue
            e, k, s = plain(rng, r, a[g], False); s = (np.exp2(3 + 5 * rng.random((len(e), 1))) * rng.random(s.shape) ** 0.5).astype(np.int64)
            i = (e[:, 0] == 200) & (np.sum(e, axis=1) == 200); k[i] = 1; s[i] = 255
            items[r][g] = e, k, s
    nq[:] = Q
    env = (np.exp2(8 * rng.random((N, 1, EV))) * rng.random((N, 128, EV))).astype(np.int64)
    return pack(rng, w, items, nq, th, env, 0.125)
def check_inputs(d):
    bad = []; x = d["ex"].astype(np.float32).reshape(N, 8, 16, W); s = d["su"].astype(np.float32).reshape(N, 8, 16, W); v = d["env"].astype(np.float32); t = d["st"]; q = d["qu"]; free = t == 0
    if np.min(t) < 0 or np.max(t) > 2: bad.append("range of st")
    if np.any(x != np.floor(x)) or np.max(x) > 200 or np.any(np.where(free[:, :, None], x != -1, x < 0)): bad.append("ex: whole numbers from 0 to 200, -1 in free places")
    if np.any(s != np.floor(s)) or np.min(s) < 0 or np.max(s) > 255 or np.any(free[:, :, None] & (s != 0)): bad.append("su: whole numbers from 0 to 255, 0 in free places")
    if np.any(v != np.floor(v)) or np.min(v) < 0 or np.max(v) > 255: bad.append("env: whole numbers from 0 to 255")
    if np.min(d["wt"]) < 0 or np.max(d["wt"]) > 4095: bad.append("range of wt")
    if np.min(d["th"]) < 1 or np.max(d["th"]) > 4080: bad.append("range of th")
    z = np.sort(q, axis=-1)
    if np.min(q) < -1 or np.max(q) >= W: bad.append("range of qu")
    if np.any((q[..., 1:] >= 0) & (q[..., :-1] < 0)): bad.append("qu: an entry behind -1")
    if np.any((q >= 0) & (np.take_along_axis(t, np.clip(q, 0, W - 1), 2) != 1)): bad.append("qu: a place that is not active")
    if np.any((z[..., 1:] == z[..., :-1]) & (z[..., 1:] >= 0)): bad.append("qu: a place twice")
    for a in range(N):
        for g in range(8):
            y = np.ascontiguousarray(x[a, g][:, ~free[a, g]].T)
            if len(y) and len(np.unique(y, axis=0)) < len(y): bad.append("ex: an index twice on rank " + str(a) + " in group " + str(g))
    return bad
def pick(t, h):
    return np.take_along_axis(t, h[:, None, :], 2)
def look(e, E, V, w):
    h1, h2, z = spots(e, w)
    f1 = np.all(pick(E, h1) == e, axis=1); f2 = np.all(pick(E, h2) == e, axis=1)
    return f1 | f2, np.where(f1[:, None], pick(V, h1), np.where(f2[:, None], pick(V, h2), 0))
def reference(ex, su, st, qu, wt, env, th):
    E = ex.astype(np.float32).astype(np.int32).reshape(N, 8, 16, W); S = su.astype(np.float32).astype(np.int32).reshape(N, 8, 16, W)
    T = st.astype(np.int32); q = qu.astype(np.int32); w = wt.astype(np.int32).reshape(N, 8, 16, 2)
    V = env.astype(np.float32).astype(np.int32).reshape(N, 8, 16, EV); t = th.astype(np.int32).reshape(N, 8, 1); one = np.eye(16, dtype=np.int32)
    for rnd in range(R):
        par = np.full((N, 8, 16, P), -1, np.int32); live = np.zeros((N, 8, P), bool)
        for a in range(N):
            s = np.where(q[a] >= 0, np.sum(pick(S[a], np.maximum(q[a], 0)), axis=1), -1)
            z = np.take_along_axis(q[a], np.argsort(-s, axis=1, kind="stable"), 1)
            live[a] = z[:, :P] >= 0; par[a] = np.where(live[a][:, None], pick(E[a], np.maximum(z[:, :P], 0)), -1)
            for g in range(8): T[a, g, z[g, :P][live[a, g]]] = 2
            q[a] = np.concatenate([z[:, P:], np.full((8, P), -1, np.int32)], axis=1)
        old = np.where(T[:, :, None, :] == 2, S, 0)
        for a in range(N):
            own = (par[a][:, :, :, None] + one[None, :, None, :]).reshape(8, 16, 16 * P)
            c = np.concatenate([own, par[a - 1] if a else np.full_like(par[0], -1)], axis=2)
            ok = np.concatenate([np.repeat(live[a], 16, axis=1), live[a - 1] if a else np.zeros_like(live[0])], axis=1)
            c = np.where(ok[:, None], c, 0)
            v = look((c[:, :, :, None] - one[None, :, None, :]).reshape(8, 16, -1), E[a], old[a], w[a])[1].reshape(8, 16, -1, 16)
            M = np.min(np.where((np.swapaxes(c, 1, 2) == 0)[:, None], 255, v), axis=3)
            good = ok & ~look(c, E[a], old[a], w[a])[0] & (np.sum(M, axis=1) >= t[a])
            good = good & (np.add.accumulate(good.astype(np.int32), axis=1) <= C)
            if a: M = np.minimum(M, look(c, E[a - 1], old[a - 1], w[a - 1])[1])
            h1, h2, z = spots(c, w[a])
            f1 = np.take_along_axis(T[a], h1, 1) == 0; f2 = np.take_along_axis(T[a], h2, 1) == 0
            to = np.where(f1, h1, np.where(f2, h2, -1)); good = good & (np.sum(M, axis=1) >= t[a]) & (to >= 0)
            new = np.abs(M - pick(V[a], z))
            for g in range(8):
                j = np.flatnonzero(good[g]); j = j[np.sort(np.unique(to[g, j], return_index=True)[1])]; p = to[g, j]
                E[a, g][:, p] = c[g][:, j]; S[a, g][:, p] = new[g][:, j]; T[a, g, p] = 1
                n = int(np.sum(q[a, g] >= 0)); m = min(len(j), Q - n); q[a, g, n:n + m] = p[:m]
    return {"ys": S.reshape(N, 128, W).astype(np.float32).astype(BF), "yst": T.astype(np.float32)}

from concourse.bass import DstId, RemoteDMATransfer
from concourse.mybir import AluOpType as A, AxisListType as AX, ActivationFunctionType as AF

B0, TOP, TW = 64, 4160, 4176
BF, F32, I32, U16 = "bfloat16", "float32", "int32", "uint16"
SB = {
    "E": (TW, BF), "S": (TW, BF), "TT": (TW, F32), "IO": (TW, F32), "EN": (1024, BF),
    "stw": (256, I32), "ex0": (256, BF), "stf": (256, F32), "sa": (256, F32), "sb": (256, F32), "e0": (256, BF),
    "qw": (12, I32), "qo": (12, U16), "qv": (12, BF), "wti": (2, I32), "w4": (4, I32), "wf": (4, F32), "wb": (4, BF),
    "th1": (8, I32), "th8": (8, I32), "thf": (8, F32), "pi": (2, I32), "col": (40, F32),
    "IG": (128, F32), "IR": (192, F32), "DI": (192, BF), "ND": (192, BF), "BLK": (256, BF), "ID": (128, BF),
    "BS": (384, BF), "LT": (128, BF), "AW": (128, BF), "LK": (2048, BF), "WM": (1024, BF), "tmp": (384, F32),
    "YP": (384, BF), "TG": (128, BF), "RS": (768, BF), "TB": (512, BF), "CP": (192, F32), "SF": (48, F32),
    "SG": (288, BF), "NB": (128, BF), "SR": (72, BF), "oc": (40, F32), "OC": (40, U16), "V12": (64, F32), "I2": (128, BF),
    "SQ": (192, BF), "KS": (192, F32), "C": (2304, BF), "PL": (192, F32), "W1": (192, F32), "W2": (192, F32),
    "pl": (2, F32), "PO": (8, U16), "NS": (64, BF), "NEc": (4, F32), "NE": (64, BF), "BI": (16, F32),
    "X0": (224, BF), "X1": (224, BF), "MB0": (192, BF), "MB1": (192, BF), "GR0": (384, BF), "GR1": (384, BF),
    "r32": (424, I32), "m32": (212, I32), "t32": (424, I32), "h32": (424, I32), "HO": (424, U16),
    "Q": (5632, BF), "sv": (352, F32), "sm": (176, F32), "SO": (176, U16), "Z": (16, F32),
    "G": (2816, BF), "MS": (3072, BF), "Y": (384, BF), "PD": (256, BF), "NQ": (768, BF),
    "rv": (48, F32), "rm": (24, F32), "RO": (24, U16), "WP": (384, BF), "NP": (384, BF),
    "PN": (384, BF), "hs": (24, F32), "fv": (24, F32), "fm": (12, I32), "z32": (12, I32), "FO": (24, U16),
    "TO": (192, F32), "EG": (208, BF), "gd": (192, BF), "cu": (192, BF), "jk": (576, BF), "ac": (4, F32),
    "CO": (4, U16), "MP": (208, BF), "DF": (96, BF), "tg": (208, F32), "U": (48, F32),
    "US": (64, F32), "KC": (52, F32), "DD": (147, F32), "dm": (4, F32), "bb": (4, BF),
    "BO": (4, U16), "XE": (48, BF),
}
SCRATCH = {k: ("sbuf", [128, v[0]], v[1]) for k, v in SB.items()}
for _i in range(8):
    SCRATCH["P%d" % _i] = ("psum", [128, 512], "float32")
NDMA = 24
SEMAPHORES = ["ev", "es", "et", "eg", "ls", "pb0", "pb1", "pu0", "pu1", "rs0", "rs1"] + ["d%d" % _i for _i in range(NDMA)]
CY = 1.04e-3
MODELS = [(1.56, 3.8, 0.1, 3.5, 3.0, 200.0), (1.04, 1.6, 0.06, 2.5, 2.0, 300.0), (2.08, 6.0, 0.06, 2.5, 2.0, 200.0), (1.56, 3.8, 0.2, 5.0, 4.0, 150.0)]
TRIES, MOVES, PLANS = 8, 6000, {}
OWN = [(0, 3), (3, 6), (6, 9), (9, 11)]
FETCH = [(0, 3, "v"), (3, 6, "v"), (6, 9, "s"), (9, 10, "s"), (10, 11, "v")]
LATE = (144, 176)
N1 = 64
NE_PAR, NE_RSP = 4, 8


def arrange(ops):
    if PLANS:
        return PLANS[0]
    n = len(ops)
    qs = [o["q"] for o in ops]
    pre = [[(d, d in o["deps"]) for d in sorted(o["deps"] | o["order"])] for o in ops]
    below = [0] * n
    for i in range(n):
        via = 0
        for d, w in pre[i]:
            if w:
                via |= below[d]
        pre[i] = [(d, w) for d, w in pre[i] if not via >> d & 1]
        below[i] = via
        for d, w in pre[i]:
            if w:
                below[i] |= 1 << d
    suc = [[] for _ in ops]
    for i in range(n):
        for d, w in pre[i]:
            suc[d].append((i, w))
    pins = [i for i in range(n) if ops[i]["lat"] < 0 and qs[i] != "g" and not ops[i]["deps"]]

    def times(m):
        cost = [(o["cost"][0] + CY * (o["cost"][1] * m[0] + o["cost"][2] * m[1])) + (m[4] if o["lat"] == 2 else 0) for o in ops]
        return cost, [m[3] if o["lat"] > 0 else o["lat"] / m[5] for o in ops], m[2]

    def replay(seq, tms):
        cost, lat, wake = tms
        idle, pipe, end, iss = {q: 0.0 for q in "vstgyx"}, 0.0, [0.0] * n, [0.0] * n
        for i in seq:
            t = idle[qs[i]]
            for d, w in pre[i]:
                t = max(t, end[d] + wake if w else (iss[d] if lat[d] < 0 else end[d]))
            iss[i] = t + cost[i]
            if qs[i] != "x":
                idle[qs[i]] = iss[i]
            if lat[i] < 0:
                pipe = max(pipe, iss[i] + 1.5) - lat[i]
                end[i] = pipe + 0.5
            else:
                end[i] = iss[i] + lat[i]
        return max(end), iss, end

    def forward(far, tms, pre, suc, fixed=None):
        cost, lat, wake = tms
        left = [len(p) for p in pre]
        ready = [0.0] * n
        cand = {q: [] for q in "vstgyx"}
        for i in range(n):
            if left[i] == 0:
                cand[qs[i]].append(i)
        idle, pipe, seq, fin = {q: 0.0 for q in cand}, 0.0, [], [0.0] * n
        while len(seq) < n:
            t0, q = min((max(idle[q], min([ready[i] for i in l])), q) for q, l in cand.items() if l)
            l = cand[q]
            now = sorted((j for j in l if ready[j] <= t0 + 1e-9), key=lambda j: -far[j])
            i = now[0]
            soon = [j for j in l if far[j] > far[i] and t0 < ready[j] < t0 + cost[i]]
            if soon:
                j = max(soon, key=lambda j: far[j])
                if max(ready[j] + far[j], ready[j] + cost[j] + far[i]) < max(t0 + far[i], t0 + cost[i] + far[j]) - 1e-9:
                    fit = [k for k in now if t0 + cost[k] <= ready[j] + 0.02]
                    i = fit[0] if fit else j
            l.remove(i)
            issue = max(idle[q], ready[i]) + cost[i]
            if q != "x":
                idle[q] = issue
            if fixed is not None:
                end = issue
            elif lat[i] < 0:
                pipe = max(pipe, issue + 1.5) - lat[i]
                end = pipe + 0.5
            else:
                end = issue + lat[i]
            fin[i] = issue
            seq.append(i)
            for j, w in suc[i]:
                if fixed is not None:
                    t = end + (wake if w else 0) + (fixed[j] if w or lat[j] >= 0 else 0)
                else:
                    t = issue if lat[i] < 0 and not w else end + (wake if w else 0)
                ready[j] = max(ready[j], t)
                left[j] -= 1
                if left[j] == 0:
                    cand[qs[j]].append(j)
        return seq, fin

    models = [times(m) for m in MODELS]
    mid = models[0]
    far = [0.0] * n
    for i in range(n - 1, -1, -1):
        far[i] = mid[0][i] + (mid[1][i] if mid[1][i] >= 0 else 2.0 - mid[1][i]) + max([far[j] + (mid[2] if w else 0) for j, w in suc[i]] + [0.0])
    best, seed = None, 1
    for it in range(TRIES):
        seq = forward(far, mid, pre, suc)[0]
        seq = pins + [i for i in seq if i not in pins]
        score = sum(replay(seq, m)[0] for m in models)
        if best is None or score < best[0]:
            best = (score, seq)
        top, iss, end = replay(seq, mid)
        far = forward(end, mid, suc, pre, [end[i] - iss[i] for i in range(n)])[1]
        far = [far[i] + (end[i] - iss[i] if not suc[i] else 0) for i in range(n)]
    score, seq = best
    for it in range(MOVES):
        seed = (seed * 1103515245 + 12345) % 2 ** 31
        k = (seed >> 8) % n
        i = seq[k]
        same = [j for j in range(max(len(pins), k - 60), min(n, k + 61)) if j != k and qs[seq[j]] == qs[i]]
        seed = (seed * 1103515245 + 12345) % 2 ** 31
        if not same or mid[1][i] < 0:
            continue
        j = same[(seed >> 8) % len(same)]
        if j < k:
            tied = {d for d, w in pre[i]}
            if any(seq[x] in tied for x in range(j, k)):
                continue
        else:
            tied = {d for d, w in suc[i]}
            if any(seq[x] in tied for x in range(k + 1, j + 1)):
                continue
        new = seq[:k] + seq[k + 1:]
        new.insert(j, i)
        sc = sum(replay(new, m)[0] for m in models)
        if sc <= score:
            score, seq = sc, new
    PLANS[0] = seq
    return seq


def rank_program(g, core, T, topo):
    rank = T.rank_of(core)
    if rank is None:
        return
    N = len(T.cores)
    ops, rec, dsem, chain, sent = [], {}, [0], {}, [0]
    Q = {"v": g.vector, "s": g.scalar, "t": g.tensor, "g": g, "y": g.sync}

    def R(name, a=0, b=None, s=1):
        b = (SB[name][0] if name in SB else 512) if b is None else b
        ap = T[name][:, a:b] if s == 1 else T[name][:, a:b:s]
        return (ap, [(name, a, b, s)])

    def IN(win, off):
        return (win[0].indirect(off[0]), win[1] + off[1])

    def meet(x, y, exact):
        if x[2] <= y[1] or y[2] <= x[1]:
            return False
        if not exact or (x[3] == 1 and y[3] == 1):
            return True
        return len(set(range(x[1], x[2], x[3])) & set(range(y[1], y[2], y[3]))) > 0

    def op(q, fn, wr, rd, tok=None, free=False, cost=(0.07, 0, 0), lat=0.0, after=(), skip=False):
        me = len(ops)
        deps, order = set(), set(after)
        for kind, rs in (("w", wr), ("r", rd)):
            for x in rs:
                psum = x[0] not in SB
                for (y, k2, i) in rec.setdefault(x[0], []):
                    o = ops[i]
                    same = o["q"] == q and o["tok"] is None and tok is None
                    if psum and not same:
                        deps.add(i)
                    elif kind == "r" and k2 == "r":
                        continue
                    elif same and q == "t":
                        order.add(i)
                    elif free and o["free"] and kind == "w" and k2 == "w":
                        continue
                    elif meet(x, y, same):
                        deps.add(i)
        for kind, rs in (("w", wr), ("r", rd)):
            for x in rs:
                rec[x[0]].append((x, kind, me))
        ops.append({"q": q, "fn": fn, "deps": deps, "tok": tok, "free": free, "order": order, "cost": cost, "lat": lat, "skip": skip})
        return me

    def regs(*xs):
        out = []
        for x in xs:
            if isinstance(x, tuple):
                out += x[1]
        return out

    def ap(x):
        return x[0] if isinstance(x, tuple) else x

    def wr_rd(o, *ins):
        return o[1][:1], o[1][1:] + regs(*ins)

    def size(x):
        n = x[1][-1]
        return len(range(n[1], n[2], n[3])) * (16 if len(x[1]) > 1 else 1)

    def tm(o, i, f=None):
        if len(o[1]) > 1:
            return (0.05, 0, size(o))
        if len(i[1]) > 1:
            return (0.06, size(i), 0)
        if f is None:
            f = 0.5 if all(SB.get(x[1][0][0], (0, F32))[1] in (BF, U16) for x in (o, i)) else 1
        return (max(64, size(i) * f) * CY, 0, 0)

    def cp(o, i):
        op("v", lambda: g.vector.tensor_copy(o[0], i[0]), *wr_rd(o, i), cost=tm(o, i))

    def tt(o, a, b, f):
        op("v", lambda: g.vector.tensor_tensor(o[0], a[0], b[0], f), *wr_rd(o, a, b),
           cost=tm(o, a, 2 if a[1][0][0] in SB and b[1][0][0] in SB else 1))

    def ts(o, a, s1, f1, s2=None, f2=None):
        if f2 is None:
            op("v", lambda: g.vector.tensor_scalar(o[0], a[0], ap(s1), None, f1), *wr_rd(o, a, s1), cost=tm(o, a))
        else:
            op("v", lambda: g.vector.tensor_scalar(o[0], a[0], ap(s1), ap(s2), f1, f2), *wr_rd(o, a, s1, s2), cost=tm(o, a))

    def ms(o, v, skip=False):
        op("v", lambda: g.vector.memset(o[0], v), o[1], [], cost=tm(o, o), skip=skip)

    def red(o, i, f, ab=False):
        op("v", lambda: g.vector.tensor_reduce(o[0], i[0], AX.X, f, apply_absolute_value=ab), *wr_rd(o, i), cost=tm(o, i, 1))

    def scan(o, d0, d1, f0, f1):
        op("v", lambda: g.vector.tensor_tensor_scan(o[0], d0[0], d1[0], 0.0, f0, f1), *wr_rd(o, d0, d1), cost=tm(o, d1))

    def act(o, i, f, bias=None, scale=1.0, acc=None):
        kw = {"scale": ap(scale)}
        if bias is not None:
            kw["bias"] = ap(bias)
        if acc is not None:
            kw["accum_out"] = acc[0]
        op("s", lambda: g.scalar.activation(o[0], i[0], f, **kw), o[1] + regs(acc), regs(i, bias, scale), cost=tm(o, i, 1))

    def get(q, o, i):
        if q == "s":
            act(o, i, AF.Copy)
        else:
            cp(o, i)

    def mm(o, l, r, start=False, stop=False):
        op("t", lambda: g.tensor.matmul(o[0], l[0], r[0], start, stop), o[1], regs(l, r), cost=tm(r, r, 1))

    def iota(o, pat, base=0, cm=0):
        cost = (0.13 + tm(o, o, 2)[0], 0, 0)
        if SB[o[1][0][0]][1] == I32:
            op("g", lambda: g.iota(o[0], pat, base, cm), o[1], [], cost=cost)
        else:
            op("g", lambda: g.iota(o[0], pat, base, cm, allow_small_or_imprecise_dtypes=True), o[1], [], cost=cost)

    def dma(q, o, i, wr, rd, kb, **kw):
        s = "d%d" % dsem[0]
        dsem[0] += 1
        chain[q] = [op(q, lambda: Q[q].dma_start(o, i, **kw).then_inc(T.sem[s], 16), wr, rd, tok=(s, 16), free=True,
                       cost=(1.0 if q == "g" else 0.05, 0, 0), lat=-kb, after=chain.get(q, []))]

    def engines(dst, first, n):
        return sum(1 << e for e in topo.engines(core, dst)[first:first + n])

    def arrive(o, sem, n, own, skip):
        op("x", None, o[1], [], tok=(sem, n), after=[own], cost=(0.0, 0, 0), skip=skip)

    def send_par(X, rnd):
        tr = []
        for k, (to, a, s) in enumerate(((rank + 1, 176, "pb"), (rank - 1, 192, "pu"))):
            if 0 <= to < N:
                rid, pid, _ = topo.addr(T.cores[to])
                tr.append(RemoteDMATransfer(dst_ids=[DstId(rid=rid, pnc=pid)], dma_engine_mask=engines(T.cores[to], NE_PAR * k, NE_PAR),
                                            remote_sem=T.sem[s + str(rnd)], src=T[X][:, 208:224], dst=T[X][:, a:a + 16]))
        sent[0] += NE_PAR * len(tr)
        return op("g", lambda: g.remote_dma_fused(tr, local_sem=T.sem.ls), [], R(X, 208, 224)[1], tok=("ls", None),
                  cost=(0.5, 0, 0), lat=1 if rnd else 2)

    def send_rsp(rnd):
        src = R("GR%d" % rnd, 176, 368)
        if rank + 1 == N:
            return op("g", None, [], src[1], tok=("ls", None), cost=(0.5, 0, 0), lat=1, skip=True)
        to = T.cores[rank + 1]
        rid, pid, _ = topo.addr(to)
        sent[0] += NE_RSP
        return op("g", lambda: g.remote_dma(T["MB%d" % rnd][:], src[0], T.sem["rs%d" % rnd], T.sem.ls, pid, rid, engines(to, 0, NE_RSP)),
                  [], src[1], tok=("ls", None), cost=(0.5, 0, 0), lat=1)

    def c(i):
        return R("col", i, i + 1)
    RC, GC, SGN, OFF, C1, C2, BASE, TH, ROOM, R16K, ACOL, AC1, DG, K512, SC, SH, SQ4, S16, TMP = 0, 1, 2, 3, 4, 5, 6, 7, 8, 9, 10, 11, 12, 13, 16, 20, 24, 28, 32
    Ew, Sw, Ep = R("E"), R("S"), R("E", B0, TOP)
    B1, B256, B8K, B16K, ID = R("BLK", 0, 128), R("BS", 0, 128), R("BS", 128, 256), R("BS", 256, 384), R("ID")

    def WM(k):
        return R("WM", 128 * k, 128 * k + 128)

    dma("s", T.wti[:], T.wt[:], R("wti")[1], [], 1)
    dma("y", T.stw[:], T.st[:], R("stw")[1], [], 128)
    dma("s", T.qw[:], T.qu[:], R("qw")[1], [], 6)
    dma("y", T.ex0[:], T.ex[0:128:16, :], R("ex0")[1], [], 64)
    dma("y", T.S[:, B0:TOP], T.su[:], R("S", B0, TOP)[1], [], 1024)
    for k in range(8):
        dma("y", T.E[16 * k + 1:16 * k + 16, B0:TOP], T.ex[16 * k + 1:16 * k + 16, :], R("E", B0, TOP)[1], [], 120)
    dma("g", T.th1[0:1, :], T.th[:], R("th1")[1], [], 1, allow_slow_non_contiguous=True)
    cp(R("stf"), R("stw"))
    ts(R("sa"), R("ex0"), -2.0, A.mult, -2.0, A.add)
    ts(R("sb"), R("stw"), 1.0, A.is_equal)
    tt(R("sa"), R("sa"), R("sb"), A.mult)
    tt(R("e0"), R("sa"), R("ex0"), A.add)
    dma("y", T.E[0:128:16, B0:TOP], T.e0[:], R("E", B0, TOP)[1], R("e0")[1], 64)
    dma("y", T.EN[:], T.env[:], R("EN")[1], [], 256)
    ops[-1]["deps"].add(len(ops) - 3)
    dma("y", T.TT[0:128:16, B0:TOP], T.stf[:], R("TT", B0, TOP)[1], R("stf")[1], 128)
    iota(R("pi", 0, 1), [[0, 1]], 0, 1)
    iota(R("IR"), [[0, 12], [1, 16]])
    iota(R("IG"), [[1, 8], [0, 16]])
    iota(R("IO", 0, 272), [[1, 272]])
    iota(R("TB", 0, 192), [[-1, 12], [-12, 16]], 255)
    iota(R("oc", 0, 11), [[1, 11]])
    iota(R("oc", 11, 22), [[1, 11]], 16)
    iota(R("tmp", 0, 128), [[0, 4], [1, 16], [0, 2]])
    iota(R("TB", 384, 448), [[-1, 64]], 255)
    op("g", lambda: g.partition_broadcast(T.th8[:], T.th1[0:1, :], 128), R("th8")[1], R("th1")[1], cost=(0.2, 0, 0))
    ms(R("S", 0, B0), 0.0)
    ms(R("S", TOP, TW), 255.0)
    ms(R("E", 0, B0), -1.0)
    ms(R("E", TOP, TW), -1.0)
    ms(R("RS"), 0.0)
    ms(R("RS", 0, 768, 16), float(2 ** 23))
    ts(R("pi", 1, 2), R("pi", 0, 1), 15, A.bitwise_and)
    ts(R("pi", 0, 1), R("pi", 0, 1), 4, A.arith_shift_right)
    cp(c(RC), R("pi", 1, 2))
    cp(c(GC), R("pi", 0, 1))
    for a, b in ((272, 544), (544, 1088), (1088, 2176), (2176, TW)):
        act(R("IO", a, b), R("IO", 0, b - a), AF.Copy, float(a))
    ms(R("IO", 63, 64), float(TW - 1))
    ts(B1, R("IG"), c(GC), A.is_equal)
    ts(R("BLK", 128, 256), R("IG"), c(GC), A.is_equal)
    ts(R("DI"), R("IR"), c(RC), A.is_equal)
    ts(R("ND"), R("IR"), c(RC), A.not_equal, float(2 ** 21), A.mult)
    ts(c(R16K), c(RC), 16384.0, A.mult)
    ms(R("CP", 0, 96), 8192.0 * 96)
    ms(R("CP", 96, 192), 8192.0 * 95)
    ts(R("qo"), R("qw"), float(B0), A.add)
    tt(ID, B1, R("DI", 0, 128), A.mult)
    ts(B256, B1, 256.0, A.mult)
    tt(R("TB", 192, 384), R("TB", 0, 192), R("ND"), A.max)
    ts(B8K, B1, 8192.0, A.mult)
    ts(B16K, B1, 16384.0, A.mult)
    ts(R("CP"), R("CP"), c(R16K), A.subtract)
    ts(c(C1), c(RC), float(TOP), A.add)
    ts(c(OFF), c(RC), 0.0, A.is_equal, -2.0, A.mult)
    ts(c(C2), c(RC), 11.0, A.is_ge, c(C1), A.mult)
    ts(c(SGN), c(OFF), 1.0, A.add)
    ts(R("w4", 0, 2), R("wti"), 4032, A.bitwise_and)
    ts(R("w4", 2, 4), R("wti"), 63, A.bitwise_and)
    cp(R("wf"), R("w4"))
    cp(R("wb"), R("w4"))
    ms(R("oc", 22, 40), 0.0)
    ms(R("YP", 352, 384), 0.0)
    ts(R("YP", 0, 176), R("DI", 0, 176), -1.0, A.mult)
    cp(R("YP", 176, 352), R("DI", 0, 176))
    ts(R("oc", 24, 32), R("oc", 24, 32), c(RC), A.add)
    ts(R("oc", 32, 40), R("oc", 32, 40), c(RC), A.add, 32.0, A.add)
    ts(R("oc", 22, 23), c(RC), 32.0, A.add)
    cp(R("OC"), R("oc"))
    ms(R("SG", 0, 144), -1.0)
    ms(R("SG", 144, 288), 0.0)
    act(R("NB"), B1, AF.Copy, 0.0, -1.0)
    for k in range(4):
        act(WM(k), B1, AF.Identity, scale=R("wf", k, k + 1))
        act(WM(4 + k), ID, AF.Identity, scale=R("wf", k, k + 1))
    ts(c(ACOL), c(RC), 32.0, A.mult, 512.0, A.add)
    ms(R("LK", 0, 1024), 0.0)
    ms(R("LK", 1024, 2048), 0.0)
    ts(c(AC1), c(RC), -32.0, A.mult, -511.0, A.add)
    ts(R("AW"), B1, c(ACOL), A.mult)
    ts(R("tmp", 128, 256), ID, c(AC1), A.mult)
    ts(c(BASE), c(RC), -32.0, A.mult, 11545.0, A.add)
    tt(R("AW"), R("AW"), R("tmp", 128, 256), A.add)
    ts(c(DG), c(RC), 256.0, A.mult, 4120.0, A.add)
    for k in range(16):
        get("vs"[k % 2], R("LK", 129 * k, 128 * k + 128, 16), R("AW", k, 128, 16))
    ts(R("tmp", 256, 384), R("tmp", 0, 128), c(RC), A.is_equal, c(DG), A.mult)
    ts(R("tmp", 0, 128), R("tmp", 0, 128), -256.0, A.mult, -4096.0, A.add)
    tt(R("TG"), R("tmp", 0, 128), R("tmp", 256, 384), A.add)
    ms(c(K512), 512.0)
    ms(R("SR"), 0.0)
    ms(R("SR", 0, 11), -1.0)
    ms(R("SR", 11, 22), 1.0)
    ms(R("SR", 24, 35), 1.0)
    ms(R("V12", 0, 48), 1.0)
    ms(R("V12", 48, 64), 2.0)
    for rnd in range(2):
        ms(R("X%d" % rnd, 176, 192), -1.0, rank != 0)
        ms(R("MB%d" % rnd), 255.0, rank != 0)
        ms(R("X%d" % rnd, 192, 208), -1.0, rank != N - 1)
    ms(R("MS", 2992, 3072), 0.0)
    ms(R("tg", 192, 208), 0.0)
    ms(R("MP", 192, 208), 0.0)
    ms(R("EG", 192, 208), 0.0)
    ms(R("KC", 48, 52), -1.0 / 128)
    ts(R("SF"), R("IO", 0, 48), 1.0 / 128, A.mult)
    ts(R("col", SC, SC + 3), R("IO", 0, 48, 16), c(RC), A.add)
    cp(R("thf"), R("th8"))
    ts(R("W2", 0, 8), R("IG", 0, 128, 16), c(GC), A.is_equal)
    ts(R("col", SH, SH + 3), R("col", SC, SC + 3), 0.5, A.add)
    ts(R("col", SQ4, SQ4 + 3), R("col", SC, SC + 3), 1.0 / 128, A.mult, -0.25, A.add)
    ts(R("col", S16, S16 + 3), R("col", SC, SC + 3), 16.0, A.add)
    tt(R("thf"), R("thf"), R("W2", 0, 8), A.mult)
    red(c(TH), R("thf"), A.add)
    ts(R("qv"), R("qw"), 0.0, A.is_ge)
    mm(R("P7", 0, 12), B1, R("qv"), True, True)
    red(c(TMP), R("P7", 0, 12), A.add)
    ts(c(ROOM), c(TMP), -1.0, A.mult, -53.0, A.add)
    ts(R("LT"), R("IR", 0, 128), c(RC), A.is_gt)
    ts(R("I2"), ID, -256.0, A.mult)
    tt(R("TB", 448, 512), R("TB", 384, 448), R("ND", 0, 64), A.max)
    tt(R("LT"), R("LT"), B1, A.mult)
    tt(R("LT"), R("LT"), R("I2"), A.add)

    mm(R("P0", 0, 192), ID, R("TB", 0, 192), True)
    mm(R("P1", 0, 192), ID, R("TB", 0, 192), True)
    mm(R("P2", 0, 192), ID, R("TB", 192, 384), True)
    cp(R("SQ"), IN(Sw, R("qo")))
    mm(R("P2", 0, 192), B256, R("SQ"), False, True)
    mm(R("P0", 0, 192), B256, R("SQ"), False, True)
    mm(R("P1", 0, 192), B256, R("SQ"), False, True)
    tt(R("PL"), IN(R("IO"), R("qo")), R("CP"), A.add)
    scan(R("KS"), R("RS", 0, 192), R("P2", 0, 192), A.add, A.min)
    for k in range(6):
        ts(R("C", 192 * k, 192 * k + 192), R("P0", 0, 192), R("KS", 16 * k + 15, 16 * k + 16), A.is_lt)
        j = k + 6
        act(R("C", 192 * j, 192 * j + 192), R("P1", 0, 192), AF.Sign, R("KS", 16 * j + 15, 16 * j + 16), -1.0)
        mm(R("P3", 0, 192), B16K, R("C", 192 * k, 192 * k + 192), k == 0)
        mm(R("P3", 0, 192), B8K, R("C", 192 * j, 192 * j + 192), False, k == 5)
    tt(R("W1"), R("P3", 0, 192), R("PL"), A.add)
    ts(R("W2"), R("W1"), -11.0 * 16384, A.add)
    red(R("pl", 1, 2), R("W2"), A.min, True)
    ts(R("PO", 4, 5), R("pl", 1, 2), c(C1), A.min, c(C2), A.max)
    ts(c(TMP + 1), R("pl", 1, 2), c(C2), A.max)
    act(R("NS", 0, 16), IN(Sw, R("PO", 4, 5)), AF.Copy)
    ts(R("PL", 0, 16), IN(R("IO"), R("PO", 4, 5)), c(R16K), A.subtract)
    ts(R("NEc", 0, 1), c(TMP + 1), float(TOP), A.is_ge, float(2 ** 22), A.mult)

    def open_hash(bank, n, sg, a):
        mm(R(bank, 0, 2 * n), WM(4), R(sg, a, a + 2 * n), True)
        mm(R(bank, 0, n), WM(6), R(sg, a, a + n))
        mm(R(bank, n, 2 * n), WM(5), R(sg, a, a + n))
        mm(R(bank, n, 2 * n), WM(7), R(sg, a, a + n))

    def weigh(bank, n, a, x, stop=False):
        for k in (0, 2, 1, 3):
            b = a + n * (k % 2)
            mm(R(bank, b, b + size(x)), WM(k), x, False, stop and k == 3)

    def homes(bank, n, a, weave):
        b = 2 * a
        cp(R("r32", b, b + 2 * n), R(bank, 0, 2 * n))
        ts(R("r32", b, b + 2 * n), R("r32", b, b + 2 * n), 4095, A.bitwise_and)
        tt(R("m32", a, a + n), R("r32", b, b + n), R("r32", b + n, b + 2 * n), A.mult)
        ts(R("t32", b, b + n), R("m32", a, a + n), 9, A.arith_shift_right)
        ts(R("t32", b + n, b + 2 * n), R("m32", a, a + n), 5, A.arith_shift_right)
        tt(R("t32", b, b + 2 * n), R("t32", b, b + 2 * n), R(bank, 0, 2 * n), A.add)
        if weave:
            ts(R("h32", b, b + 2 * n, 2), R("t32", b, b + n), 4095, A.bitwise_and)
            ts(R("h32", b + 1, b + 2 * n, 2), R("t32", b + n, b + 2 * n), 4095, A.bitwise_and)
        else:
            ts(R("h32", b, b + 2 * n), R("t32", b, b + 2 * n), 4095, A.bitwise_and)
        cp(R("HO", b, b + 2 * n), R("h32", b, b + 2 * n))

    def across(bank, n, src, a, start):
        for k in range(16):
            mm(R(bank, 0, n), R("LK", 128 * k, 128 * k + 128), R(src, a + k, a + 16 * n, 16), start and k == 0, k == 15)

    for rnd in range(2):
        X, MB, GR = "X%d" % rnd, "MB%d" % rnd, "GR%d" % rnd
        po = R("PO", 2 * rnd, 2 * rnd + 1)
        open_hash("P0", N1, "SG", 144 - N1)
        open_hash("P1", 176 - N1, "SG", N1 - 32)
        red(R("pl", 0, 1), R("W1", 0, 64 if rnd else 192), A.min, True)
        ts(po, R("pl", 0, 1), c(C1), A.min, c(C2), A.max)
        ts(R(X, 208, 224), IN(Ew, po), c(SGN), A.mult, c(OFF), A.add)
        own = send_par(X, rnd)
        tt(R(X, 0, 64), IN(R(X, 208, 224), R("OC", 0, 4)), R("YP", 176, 240), A.add)
        tt(R(X, 64, 176), IN(R(X, 208, 224), R("OC", 4, 11)), R("YP", 240, 352), A.add)
        weigh("P0", N1, 0, R(X, 0, N1), True)
        weigh("P1", 176 - N1, 0, R(X, N1, 176), True)
        act(R("BI"), R(X, 208, 224), AF.Copy, -1.0, -4.0)
        cp(IN(Ew, po), R(X, 208, 224))
        cp(IN(R("TT"), po), R("V12", 48, 64))
        homes("P0", N1, 0, True)
        homes("P1", 176 - N1, N1, True)
        ts(R("P1", 320, 496), R(X, 0, 176), 0.0, A.is_equal, float(2 ** 20), A.mult)
        tt(R("h32", 0, 352, 2), R("h32", 0, 352, 2), R("P1", 320, 496), A.add)
        open_hash("P2", 36, "SR", 0)
        weigh("P2", 36, 24, R(X, 208, 219))
        arrive(R(X, 176, 192), "pb%d" % rnd, NE_PAR, own, rank == 0)
        arrive(R(X, 192, 208), "pu%d" % rnd, NE_PAR, own, rank == N - 1)
        Xr = R(X, 176, 224)
        tt(R("PD"), IN(Xr, R("OC", 24, 40)), R("BLK"), A.mult)
        weigh("P2", 36, 0, R(X, 176, 187))
        weigh("P2", 36, 11, R(X, 192, 203))
        for k in range(4):
            b = 36 * (k % 2)
            mm(R("P2", b + 22, b + 23), R("PD", 128, 256), R("wb", k, k + 1))
            mm(R("P2", b + 35, b + 36), R("PD", 0, 128), R("wb", k, k + 1), False, k == 3)
        tt(R("Y"), IN(Xr, R("OC", 0, 24)), R("YP"), A.add)
        homes("P2", 36, 176, False)
        tt(R("NQ", 0, 384), IN(Ep, R("HO", 352, 376)), R("Y"), A.not_equal)
        tt(R("NQ", 384, 768), IN(Ep, R("HO", 388, 412)), R("Y"), A.not_equal)
        across("P6", 48, "NQ", 0, True)
        ts(R("Z", 0, 11), R(X, 176, 187), 0.0, A.is_equal, float(2 ** 20), A.mult)
        ts(R("z32"), R("m32", 200, 212), 7, A.arith_shift_right, 1023, A.bitwise_and)
        ts(R("hs", 0, 12), R("h32", 376, 388), float(B0), A.add)
        ts(R("hs", 12, 24), R("h32", 412, 424), float(B0 + 8192), A.add)
        tt(R("h32", 352, 363), R("h32", 352, 363), R("Z", 0, 11), A.add)
        cp(R("FO", 12, 24), R("z32"))
        ts(R("P6", 0, 48), R("P6", 0, 48), 0.0, A.not_equal, 8192.0, A.mult)
        tt(R("rv", 0, 24), R("h32", 352, 376), R("P6", 0, 24), A.subtract)
        tt(R("rv", 24, 48), R("h32", 388, 412), R("P6", 24, 48), A.subtract)
        tt(R("rm"), R("rv", 0, 24), R("rv", 24, 48), A.max)
        ts(R("RO"), R("rm"), float(B0), A.add, float(TOP), A.min)
        get("s", R(GR), IN(Sw, R("RO")))
        own = send_rsp(rnd)
        scan(R("MS", 2816, 2992), R("RS", 0, 176), R(GR, 0, 176), A.add, A.min)
        act(R("WP", 0, 192), IN(Ep, R("HO", 376, 388)), AF.Abs, 1.0)
        act(R("WP", 192, 384), IN(Ep, R("HO", 412, 424)), AF.Abs, 1.0)
        across("P2", 24, "WP", 0, True)
        act(R("P7", 0, 192), R(X, 0, 192), AF.Copy, 1.0)
        tt(R("NP", 0, 192), R("WP", 0, 192), R("P7", 0, 192), A.not_equal)
        tt(R("NP", 192, 384), R("WP", 192, 384), R("P7", 0, 192), A.not_equal)
        mm(R("P7", 0, 384), B1, R("NP"), True, True)
        act(R("PN"), R("P7", 0, 384), AF.Relu, c(K512), -512.0)
        mm(R("P5", 0, 192), R("NB"), R("PN", 0, 192), True)
        mm(R("P5", 0, 192), R("NB"), R("PN", 192, 384))
        ts(R("fv"), R("P2", 0, 24), 0.0, A.is_equal)
        tt(R("fv"), R("fv"), R("hs"), A.mult)
        tt(R("fm"), R("fv", 0, 12), R("fv", 12, 24), A.max)
        ts(R("fm"), R("fm"), 8191, A.bitwise_and)
        cp(R("FO", 0, 12), R("fm"))
        act(R("EG", 0, 192), IN(R("EN"), R("FO", 12, 24)), AF.Copy)
        act(R("TO"), IN(R("IO"), R("FO", 0, 12)), AF.Copy)
        for i, (a, b) in enumerate(OWN):
            n, bank = 32 * (b - a), "P%d" % (3 + i % 2)
            mm(R(bank, 0, n), ID, R("TG", 0, n), True)
            for p in range(a, b):
                act(R("Q", 512 * p, 512 * p + 512), IN(Ep, R("HO", 32 * p, 32 * p + 32)), AF.Square, R("BI", p, p + 1), 4.0)
            across(bank, n, "Q", 512 * a, False)
            ts(R(bank, 0, n), R(bank, 0, n), c(BASE), A.not_equal, 8192.0, A.mult)
            tt(R("sv", 32 * a, 32 * b), R("h32", 32 * a, 32 * b), R(bank, 0, n), A.subtract)
            tt(R("sm", 16 * a, 16 * b), R("sv", 32 * a, 32 * b, 2), R("sv", 32 * a + 1, 32 * b, 2), A.max)
            ts(R("SO", 16 * a, 16 * b), R("sm", 16 * a, 16 * b), float(B0), A.add, float(TOP), A.min)
        for a, b, q in FETCH:
            get(q, R("G", 256 * a, 256 * b), IN(Sw, R("SO", 16 * a, 16 * b)))
            scan(R("MS", 256 * a, 256 * b), R("RS", 0, 256 * (b - a)), R("G", 256 * a, 256 * b), A.add, A.min)
        arrive(R(MB), "rs%d" % rnd, NE_RSP, own, rank == 0)
        parts = ((LATE[1], 192, "P7"), (0, LATE[0], "P7"), (LATE[0], LATE[1], "P6"))
        for a, b, bank in parts:
            mm(R("P5", a, b), B1, R("MS", 16 * a + 15, 16 * b, 16), False, a == LATE[0])
        ts(R("gd"), R("P5", 0, 192), c(TH), A.is_ge)
        scan(R("cu"), R("gd"), R("gd"), A.add, A.max)
        for t in range(3):
            act(R("jk", 192 * t, 192 * t + 192), R("cu"), AF.Sign, c(SH + t), -1.0, R("ac", t, t + 1))
        for a, b, bank in parts:
            tt(R("MP", a, b), R("MS", 16 * a + 15, 16 * b, 16), R(MB, a, b), A.min)
            mm(R(bank, a, b), B1, R("MP", a, b), True, True)
            ts(R(bank, a, b), R(bank, a, b), c(TH), A.is_ge, 8192.0, A.mult)
            tt(R("tg", a, b), R("TO", a, b), R(bank, a, b), A.min)
        if rnd == 0:
            mm(R("P0", 0, 64), ID, R("TB", 384, 448), True)
            mm(R("P2", 0, 64), ID, R("TB", 448, 512), True)
        ts(R("CO", 0, 3), R("ac", 0, 3), 0.5, A.mult, 96.0, A.add)
        co, bo = R("CO", 0, 3), R("BO", 0, 3)
        tt(R("U"), IN(R("tg"), co), R("ND", 0, 48), A.max)
        act(R("DF", 0, 48), IN(R("EG"), co), AF.Copy)
        tt(R("KC", 0, 48), IN(R("tg"), co), R("SF"), A.add)
        tt(R("DF", 48, 96), IN(R("MP"), co), R("DF", 0, 48), A.subtract)
        act(R("NS", 16, 64), R("DF", 48, 96), AF.Abs)
        scan(R("US", 0, 48), R("RS", 0, 48), R("U"), A.add, A.min)
        for t in range(3):
            ts(R("DD", 49 * t, 49 * t + 49), R("KC", 0, 49), R("US", 16 * t + 15, 16 * t + 16), A.subtract, c(SQ4 + t), A.subtract)
            red(R("dm", t, t + 1), R("DD", 49 * t, 49 * t + 49), A.min, True)
        ts(R("bb", 0, 3), R("dm", 0, 3), 0.25, A.is_ge)
        for t in range(3):
            ts(R("BO", t, t + 1), R("bb", t, t + 1), R("US", 16 * t + 15, 16 * t + 16), A.mult, c(S16 + t), A.max)
        if rnd == 0:
            mm(R("P2", 0, 64), B256, R("NS"), False, True)
            mm(R("P0", 0, 64), B256, R("NS"), False, True)
            mm(R("P7", 0, 3), R("LT"), R("bb", 0, 3), True)
            mm(R("P7", 1, 3), B1, R("bb", 0, 2))
            mm(R("P7", 2, 3), B1, R("bb", 0, 1), False, True)
            scan(R("KS", 0, 64), R("RS", 0, 64), R("P2", 0, 64), A.add, A.min)
            ts(R("NEc", 1, 4), R("P7", 0, 3), c(ROOM), A.is_ge, float(2 ** 22), A.mult)
            ts(R("XE"), IN(R(X), co), c(SGN), A.mult, c(OFF), A.add)
            for t in range(4):
                ts(R("C", 64 * t, 64 * t + 64), R("P0", 0, 64), R("NEc", t, t + 1), A.add, R("KS", 16 * t + 15, 16 * t + 16), A.is_lt)
                act(R("NE", 16 * t, 16 * t + 16), R("DI", 0, 16), AF.Identity, scale=R("NEc", t, t + 1))
            for t in range(4):
                mm(R("P3", 0, 64), B16K, R("C", 64 * t, 64 * t + 64), t == 0)
            mm(R("P3", 0, 64), B1, R("NE"), False, True)
            ts(R("PL", 16, 64), R("KC", 0, 48), c(R16K), A.subtract)
            cp(IN(Ew, bo), R("XE"))
            tt(R("W1", 0, 64), R("P3", 0, 64), R("PL", 0, 64), A.add)
        cp(IN(Sw, bo), R("NS", 16, 64))
        cp(IN(R("TT"), bo), R("V12", 0, 48))
    dma("y", T.ys[:], T.S[:, B0:TOP], [], R("S")[1], 1024)
    dma("s", T.yst[:], T.TT[0:128:16, B0:TOP], [], R("TT")[1], 128)

    seq = [i for i in arrange(ops) if not ops[i]["skip"]]
    at = {i: k for k, i in enumerate(seq)}
    need, last, plan = set(), {}, {}
    for i in seq:
        o = ops[i]
        if o["q"] == "x":
            continue
        best = {}
        for d in o["deps"]:
            p = ops[d]
            if not p["skip"]:
                key = p["tok"][0] if p["tok"] else p["q"]
                best[key] = max(best.get(key, -1), at[d])
        plan[i] = []
        for key, d in sorted(best.items()):
            if last.get((o["q"], key), -1) < d:
                last[(o["q"], key)] = d
                plan[i].append(seq[d])
                need.add(seq[d])
    count = {"v": 0, "s": 0, "t": 0, "g": 0}
    token = {}
    for i in seq:
        o = ops[i]
        if o["q"] == "x":
            token[i] = o["tok"]
            continue
        for d in plan[i]:
            Q[o["q"]].wait_ge(T.sem[token[d][0]], token[d][1])
        r = o["fn"]()
        if o["tok"] is not None:
            token[i] = o["tok"]
        elif i in need:
            count[o["q"]] += 1
            token[i] = ("e" + o["q"], count[o["q"]])
            r.then_inc(T.sem[token[i][0]], 1)
    for i in seq:
        o = ops[i]
        if o["tok"] is not None and o["tok"][1] is not None and i not in need:
            g.wait_ge(T.sem[o["tok"][0]], o["tok"][1])
    g.wait_ge(T.sem.ls, sent[0])
